import numpy as np, ml_dtypes
CORES = [7,391,135,263,15,399,143,271]
N = 8
import mx_ref
NC = 128
BF = ml_dtypes.bfloat16
def cut(t, i, w=512):
    return t[:, w * i:w * i + w]
def term(a, B):
    return np.stack([np.maximum(mx_ref.matmul(mx_ref.quantize(cut(a, i)), B), 0) for i in range(4)], axis=2).reshape(128, -1)
def setup_inputs(rng):
    def f(*shape):
        return mx_ref.flush((rng.standard_normal(shape, dtype=np.float32) * np.exp2(rng.integers(-2, 3, shape[:-1] + (1,)))).astype(BF))
    return {"a": f(N, 128, 4 * 512), "b": f(N, 128, 4 * NC)}
def setup_inputs_blocks(rng):
    d = setup_inputs(rng)
    for k in ("a", "b"): d[k] = mx_ref.spread(d[k], rng, 2)
    return d
def setup_inputs_wide(rng):
    d = setup_inputs(rng)
    for k in ("a", "b"): d[k] = mx_ref.flush((d[k].astype(np.float32) * np.exp2(rng.integers(-4, 5, (N, 1, 1))).astype(np.float32)).astype(BF))
    return d
def setup_inputs_lossless(rng):
    a = np.zeros((N, 128, 4 * 128, 4), np.float32)
    for r in range(N):
        k = rng.integers(0, 512, size=4 * 128)
        a[r, k // 4, np.arange(4 * 128), k % 4] = 1.0
    size = np.repeat(2.0 ** rng.integers(-4, 5, size=(1, 1, (4 * NC) // 4)), 4, axis=2)
    b = (rng.random((N, 128, 4 * NC)) < 0.8) * size
    return {"a": a.reshape(N, 128, 4 * 512).astype(BF), "b": b.astype(np.float32).astype(BF)}
def reference(a, b):
    Bq = [mx_ref.quantize(b[c]) for c in range(N)]
    y = np.zeros((N, 128, 4 * NC), np.float32)
    for c in range(N):
        y[c] = mx_ref.total([term(a[r], Bq[c]) for r in range(N)])
    return {"y": y}

@@ -1,0 +1,182 @@
+from concourse.bass import DstId, RemoteDMATransfer
+from concourse.mybir import dt, AluOpType, ActivationFunctionType
+
+SCRATCH = {
+    "a_in": ("sbuf", [128, 2048], "bfloat16"),
+    "b_in": ("sbuf", [128, 512], "bfloat16"),
+    "aq": ("sbuf", [128, 512], "float8_e4m3fn_x4"),
+    "as_": ("sbuf", [128, 512], "uint8"),
+    "pq": ("sbuf", [128, 512], "float8_e4m3fn_x4"),
+    "ps": ("sbuf", [128, 512], "uint8"),
+    "bq": ("sbuf", [128, 512], "float8_e4m3fn_x4"),
+    "bs": ("sbuf", [128, 512], "uint8"),
+    "ones": ("sbuf", [128, 516], "bfloat16"),
+    "w": ("sbuf", [128, 516], "bfloat16"),
+    "sq": ("sbuf", [128, 512], "float8_e4m3fn_x4"),
+    "ss": ("sbuf", [128, 512], "uint8"),
+    "h1": ("sbuf", [128, 2048], "bfloat16"),
+    "h1q": ("sbuf", [128, 512], "float8_e4m3fn_x4"),
+    "h1s": ("sbuf", [128, 512], "uint8"),
+    "h2": ("sbuf", [128, 1536], "bfloat16"),
+    "h2q": ("sbuf", [128, 384], "float8_e4m3fn_x4"),
+    "h2s": ("sbuf", [128, 384], "uint8"),
+    "uq": ("sbuf", [128, 384], "float8_e4m3fn_x4"),
+    "us": ("sbuf", [128, 384], "uint8"),
+    "loc": ("sbuf", [128, 512], "float32"),
+    "yout": ("sbuf", [128, 512], "float32"),
+    "pa": ("psum", [128, 2048], "float32"),
+    "pb": ("psum", [128, 2048], "float32"),
+}
+SEMAPHORES = (["lb", "la0", "la1", "ones", "wsel", "bqd", "aqd0", "aqd1", "sqd", "barr", "parr0", "parr1",
+               "h1d", "h2m", "h2d", "locd", "yd", "st", "sent"]
+              + ["p1_%d" % i for i in range(4)] + ["r1_%d" % i for i in range(4)] + ["p2_%d" % i for i in range(4)]
+              + ["u_%d" % i for i in range(4)] + ["t_%d" % k for k in range(3)])
+
+
+def rank_program(g, core, T, topo):
+    if T.rank_of(core) is None:
+        return
+    S = T.sem
+    rack = topo.rack(topo.host(core))
+    near = [None, None, None]
+    far = None
+    for d in T.cores:
+        if d == core:
+            continue
+        if topo.rack(topo.host(d)) == rack:
+            near[0 if topo.mates(core, d) else 1 if topo.same_plane(core, d) else 2] = d
+        elif topo.chip(d) == topo.chip(core) and topo.may_write(core, d):
+            far = d
+
+    def engines(d):
+        m = topo.mask(core, d)
+        return [e for e in range(16) if m >> e & 1]
+
+    def bits(es):
+        return sum(1 << e for e in es)
+
+    def dst(d):
+        rid, pid = topo.addr(d, core)
+        return DstId(rid=rid, pnc=pid)
+
+    def codes(t, lo, hi):
+        return t[:, lo:hi].bitcast(dt.uint8)
+
+    sent = [0]
+
+    def to_far(out, in_, sem):
+        rid, pid = topo.addr(far, core)
+        es = engines(far)
+        g.remote_dma(out, in_, sem, S.sent, pid, rid, bits(es))
+        sent[0] += len(es)
+
+    g.sync.dma_start(T.b_in[:], T.b[:]).then_inc(S.lb, 16)
+    g.scalar.dma_start(T.a_in[:, 0:1024], T.a[:, 0:1024]).then_inc(S.la0, 16)
+    g.sync.dma_start(T.a_in[:, 1024:2048], T.a[:, 1024:2048]).then_inc(S.la1, 16)
+
+    v = g.vector
+    v.memset(T.ones[:], 1.0).then_inc(S.ones, 1)
+    v.wait_ge(S.lb, 16)
+    v.quantize_mx(T.bq[:, 384:512], T.bs[:, 384:512], T.b_in[:]).then_inc(S.bqd, 1)
+    v.wait_ge(S.la0, 16)
+    v.quantize_mx(T.aq[:, 0:256], T.as_[:, 0:256], T.a_in[:, 0:1024]).then_inc(S.aqd0, 1)
+    v.wait_ge(S.la1, 16)
+    v.quantize_mx(T.aq[:, 256:512], T.as_[:, 256:512], T.a_in[:, 1024:2048]).then_inc(S.aqd1, 1)
+    v.wait_ge(S.wsel, 1)
+    for i in range(4):
+        v.quantize_mx(T.sq[:, 128 * i:128 * i + 128], T.ss[:, 128 * i:128 * i + 128],
+                      T.w[:, 3 - i:515 - i]).then_inc(S.sqd, 1)
+
+    g.wait_ge(S.ones, 1)
+    g.affine_select(T.w[:], T.ones[:], [[-1, 516]], AluOpType.is_equal, 0.0, 3, 4).then_inc(S.wsel, 1)
+    es = engines(near[0])
+    ids = [dst(d) for d in near]
+    g.wait_ge(S.bqd, 1)
+    g.remote_dma_fused([RemoteDMATransfer(
+        dst_ids=ids, dma_engine_mask=bits(es), remote_sem=S.barr, srcs=[codes(T.bq, 384, 512)],
+        dsts=[codes(T.bq, 128 * k, 128 * k + 128) for k in range(3)])], local_sem=S.sent)
+    g.remote_dma_fused([RemoteDMATransfer(
+        dst_ids=ids, dma_engine_mask=bits(es), remote_sem=S.barr, srcs=[T.bs[:, 384:512]],
+        dsts=[T.bs[:, 128 * k:128 * k + 128] for k in range(3)])], local_sem=S.sent)
+    sent[0] += 2 * len(es)
+    nb = 6 * len(es)
+    g.wait_ge(S.aqd0, 1)
+    g.wait_ge(S.aqd1, 1)
+    to_far(T.ps[:], T.as_[:], S.parr0)
+    to_far(codes(T.pq, 0, 256), codes(T.aq, 0, 256), S.parr0)
+    to_far(codes(T.pq, 256, 512), codes(T.aq, 256, 512), S.parr1)
+    nf = len(engines(far))
+
+    t = g.tensor
+    t.wait_ge(S.bqd, 1)
+    t.wait_ge(S.aqd0, 1)
+    t.wait_ge(S.aqd1, 1)
+    t.wait_ge(S.barr, nb)
+    for i in range(4):
+        c = slice(128 * i, 128 * i + 128)
+        t.matmul_mx(T.pa[:, 512 * i:512 * i + 512], T.aq[:, c], T.as_[:, c], T.bq[:], T.bs[:], True, True
+                    ).then_inc(S["p1_%d" % i], 1)
+    for i in range(4):
+        src, out = T.pa[:, 512 * i:512 * i + 512], T.h1[:, i:2048:4]
+        if i % 2 == 0:
+            g.scalar.wait_ge(S["p1_%d" % i], 1)
+            g.scalar.activation(out, src, ActivationFunctionType.Relu).then_inc(S["r1_%d" % i], 1)
+        else:
+            v.wait_ge(S["p1_%d" % i], 1)
+            v.tensor_scalar(out, src, 0.0, None, AluOpType.max).then_inc(S["r1_%d" % i], 1)
+    for i in range(4):
+        v.wait_ge(S["r1_%d" % i], 1)
+    v.quantize_mx(T.h1q[:], T.h1s[:], T.h1[:]).then_inc(S.h1d, 1)
+    t.wait_ge(S.sqd, 4)
+    t.wait_ge(S.h1d, 1)
+    for i in range(4):
+        c = slice(128 * i, 128 * i + 128)
+        t.matmul_mx(T.pb[:, 512 * i:512 * i + 512], T.sq[:, c], T.ss[:, c], T.h1q[:], T.h1s[:], True, False)
+    for i in range(4):
+        if i == 0:
+            t.wait_ge(S.parr0, 2 * nf)
+        if i == 2:
+            t.wait_ge(S.parr1, nf)
+        c = slice(128 * i, 128 * i + 128)
+        t.matmul_mx(T.pb[:, 512 * i:512 * i + 512], T.pq[:, c], T.ps[:, c], T.bq[:], T.bs[:], False, True
+                    ).then_inc(S["p2_%d" % i], 1)
+    for i in range(4):
+        v.wait_ge(S["p2_%d" % i], 1)
+        v.tensor_tensor(T.h2[:, i:1536:4], T.pb[:, 512 * i:512 * i + 384], T.h1[:, i:1536:4], AluOpType.max
+                        ).then_inc(S.h2m, 1)
+    v.wait_ge(S.h2m, 4)
+    v.quantize_mx(T.h2q[:], T.h2s[:], T.h2[:]).then_inc(S.h2d, 1)
+    for i in range(4):
+        v.tensor_tensor(T.loc[:, i:512:4], T.pb[:, 512 * i + 384:512 * i + 512], T.h1[:, 1536 + i:2048:4], AluOpType.max
+                        ).then_inc(S.locd, 1)
+
+    mc = [es[0:4], es[4:6], es[6:8]]
+    mp = [es[4:8], es[0:2], es[2:4]]
+    g.wait_ge(S.h2d, 1)
+    for part, masks in ((0, mc), (1, mp)):
+        tr = []
+        for k in range(3):
+            lo, hi = 128 * k, 128 * k + 128
+            s, d = (codes(T.h2q, lo, hi), codes(T.uq, lo, hi)) if part == 0 else (T.h2s[:, lo:hi], T.us[:, lo:hi])
+            tr.append(RemoteDMATransfer(dst_ids=[ids[k]], dma_engine_mask=bits(masks[k]), remote_sem=S["t_%d" % k],
+                                        srcs=[s], dsts=[d]))
+            sent[0] += len(masks[k])
+        g.remote_dma_fused(tr, local_sem=S.sent)
+
+    for k in range(3):
+        t.wait_ge(S["t_%d" % k], len(mc[k]) + len(mp[k]))
+        u = slice(128 * k, 128 * k + 128)
+        for i in range(4):
+            c = slice(128 * i, 128 * i + 128)
+            m = t.matmul_mx(T.pa[:, 512 * i:512 * i + 128], T.sq[:, c], T.ss[:, c], T.uq[:, u], T.us[:, u], k == 0, k == 2)
+            if k == 2:
+                m.then_inc(S["u_%d" % i], 1)
+    v.wait_ge(S.locd, 4)
+    for i in range(4):
+        v.wait_ge(S["u_%d" % i], 1)
+        v.tensor_tensor(T.yout[:, i:512:4], T.pa[:, 512 * i:512 * i + 128], T.loc[:, i:512:4], AluOpType.add
+                        ).then_inc(S.yd, 1)
+    g.sync.wait_ge(S.yd, 4)
+    g.sync.dma_start(T.y[:], T.yout[:]).then_inc(S.st, 16)
+    g.sync.wait_ge(S.st, 16)
+    g.wait_ge(S.sent, sent[0])

@@ -14,9 +14,8 @@ SCRATCH = {
     "w": ("sbuf", [128, 516], "bfloat16"),
     "sq": ("sbuf", [128, 512], "float8_e4m3fn_x4"),
     "ss": ("sbuf", [128, 512], "uint8"),
-    "h1": ("sbuf", [128, 2048], "bfloat16"),
-    "h1q": ("sbuf", [128, 512], "float8_e4m3fn_x4"),
-    "h1s": ("sbuf", [128, 512], "uint8"),
+    "r1": ("sbuf", [128, 2048], "float32"),
+    "r2": ("sbuf", [128, 2048], "float32"),
     "h2": ("sbuf", [128, 1536], "bfloat16"),
     "h2q": ("sbuf", [128, 384], "float8_e4m3fn_x4"),
     "h2s": ("sbuf", [128, 384], "uint8"),
@@ -27,48 +26,87 @@ SCRATCH = {
     "pa": ("psum", [128, 2048], "float32"),
     "pb": ("psum", [128, 2048], "float32"),
 }
-SEMAPHORES = (["lb", "la0", "la1", "ones", "wsel", "bqd", "aqd0", "aqd1", "sqd", "barr", "parr0", "parr1",
-               "h1d", "h2m", "h2d", "locd", "yd", "st", "sent"]
-              + ["p1_%d" % i for i in range(4)] + ["r1_%d" % i for i in range(4)] + ["p2_%d" % i for i in range(4)]
-              + ["u_%d" % i for i in range(4)] + ["t_%d" % k for k in range(3)])
+SEMAPHORES = (["lb", "la0", "la1", "ones", "wsel", "bqd", "aqd0", "aqd1", "sqd", "barr", "parr0",
+               "h2m", "h2d", "locd", "yd", "st", "sent", "ro", "hb0", "hb1", "ha0", "ha1"]
+              + ["%s_%d" % (n, i) for n in ("p1", "r1", "p2", "r2", "u", "parr") for i in range(4)]
+              + ["t_%d" % k for k in range(3)])
+ORDER = (2, 3, 0, 1)
+
+
+def around(r, T, topo):
+    near, far = [None, None, None], None
+    for d in T.cores:
+        if d == r:
+            continue
+        if topo.rack(topo.host(d)) == topo.rack(topo.host(r)):
+            near[0 if topo.mates(r, d) else 1 if topo.same_plane(r, d) else 2] = d
+        elif topo.chip(d) == topo.chip(r) and topo.may_write(r, d):
+            far = d
+    chip = [c for c in range(r - 128 if r > 128 else 0, r + 128)
+            if topo.host(c) == topo.host(r) and topo.chip(c) == topo.chip(r) and c != r]
+    ha = [c for c in chip if topo.die(c) == topo.die(r) and topo.may_write(c, near[1])][0]
+    hb = [c for c in chip if topo.die(c) != topo.die(r) and topo.may_write(c, near[2])][0]
+    return near, far, (ha, hb)
+
+
+def bits(es):
+    return sum(1 << e for e in es)
+
+
+def codes(t, lo, hi):
+    return t[:, lo:hi].bitcast(dt.uint8)
+
+
+def helper(g, core, T, topo):
+    S = T.sem
+    for r in T.cores:
+        if topo.host(r) != topo.host(core) or topo.chip(r) != topo.chip(core):
+            continue
+        near, far, hs = around(r, T, topo)
+        if core not in hs:
+            continue
+        k = hs.index(core)
+        sent = 0
+        lo = 128 * k
+        n = 4
+        for sem, d, out, in_, rs in (
+                (S.hb0, near[1 + k], codes(T.bq, 128 + lo, 256 + lo), codes(T.bq, 384, 512), S.barr),
+                (S.hb1, near[1 + k], T.bs[:, 128 + lo:256 + lo], T.bs[:, 384:512], S.barr),
+                (S.ha0, far, codes(T.pq, lo, lo + 128), codes(T.aq, lo, lo + 128), S["parr_%d" % k]),
+                (S.ha1, far, T.ps[:, lo:lo + 128], T.as_[:, lo:lo + 128], S["parr_%d" % k])):
+            g.wait_ge(sem, n)
+            rid, pid = topo.addr(d, core)
+            m = topo.mask(core, d)
+            g.remote_dma(out, in_, rs, S.sent, pid, rid, m)
+            sent += sum(m >> e & 1 for e in range(16))
+        g.wait_ge(S.sent, sent)
 
 
 def rank_program(g, core, T, topo):
     if T.rank_of(core) is None:
+        helper(g, core, T, topo)
         return
     S = T.sem
-    rack = topo.rack(topo.host(core))
-    near = [None, None, None]
-    far = None
-    for d in T.cores:
-        if d == core:
-            continue
-        if topo.rack(topo.host(d)) == rack:
-            near[0 if topo.mates(core, d) else 1 if topo.same_plane(core, d) else 2] = d
-        elif topo.chip(d) == topo.chip(core) and topo.may_write(core, d):
-            far = d
+    near, far, hs = around(core, T, topo)
 
     def engines(d):
         m = topo.mask(core, d)
         return [e for e in range(16) if m >> e & 1]
 
-    def bits(es):
-        return sum(1 << e for e in es)
-
     def dst(d):
         rid, pid = topo.addr(d, core)
         return DstId(rid=rid, pnc=pid)
 
-    def codes(t, lo, hi):
-        return t[:, lo:hi].bitcast(dt.uint8)
-
+    es = engines(near[0])
+    on = [e for e in engines(hs[0]) if e not in es]
     sent = [0]
 
-    def to_far(out, in_, sem):
-        rid, pid = topo.addr(far, core)
-        es = engines(far)
-        g.remote_dma(out, in_, sem, S.sent, pid, rid, bits(es))
-        sent[0] += len(es)
+    def send(transfers):
+        tr = []
+        for d, mask, sem, out, in_ in transfers:
+            tr.append(RemoteDMATransfer(dst_ids=[dst(d)], dma_engine_mask=bits(mask), remote_sem=sem, srcs=[in_], dsts=[out]))
+            sent[0] += len(mask)
+        g.remote_dma_fused(tr, local_sem=S.sent)
 
     g.sync.dma_start(T.b_in[:], T.b[:]).then_inc(S.lb, 16)
     g.scalar.dma_start(T.a_in[:, 0:1024], T.a[:, 0:1024]).then_inc(S.la0, 16)
@@ -82,92 +120,98 @@ def rank_program(g, core, T, topo):
     v.quantize_mx(T.aq[:, 0:256], T.as_[:, 0:256], T.a_in[:, 0:1024]).then_inc(S.aqd0, 1)
     v.wait_ge(S.la1, 16)
     v.quantize_mx(T.aq[:, 256:512], T.as_[:, 256:512], T.a_in[:, 1024:2048]).then_inc(S.aqd1, 1)
-    v.wait_ge(S.wsel, 1)
-    for i in range(4):
-        v.quantize_mx(T.sq[:, 128 * i:128 * i + 128], T.ss[:, 128 * i:128 * i + 128],
-                      T.w[:, 3 - i:515 - i]).then_inc(S.sqd, 1)
 
-    g.wait_ge(S.ones, 1)
-    g.affine_select(T.w[:], T.ones[:], [[-1, 516]], AluOpType.is_equal, 0.0, 3, 4).then_inc(S.wsel, 1)
-    es = engines(near[0])
-    ids = [dst(d) for d in near]
     g.wait_ge(S.bqd, 1)
-    g.remote_dma_fused([RemoteDMATransfer(
-        dst_ids=ids, dma_engine_mask=bits(es), remote_sem=S.barr, srcs=[codes(T.bq, 384, 512)],
-        dsts=[codes(T.bq, 128 * k, 128 * k + 128) for k in range(3)])], local_sem=S.sent)
-    g.remote_dma_fused([RemoteDMATransfer(
-        dst_ids=ids, dma_engine_mask=bits(es), remote_sem=S.barr, srcs=[T.bs[:, 384:512]],
-        dsts=[T.bs[:, 128 * k:128 * k + 128] for k in range(3)])], local_sem=S.sent)
-    sent[0] += 2 * len(es)
+    send([(hs[0], on[0:4], S.hb0, codes(T.bq, 384, 512), codes(T.bq, 384, 512)),
+          (hs[1], on[4:8], S.hb0, codes(T.bq, 384, 512), codes(T.bq, 384, 512)),
+          (near[0], es, S.barr, codes(T.bq, 0, 128), codes(T.bq, 384, 512))])
+    send([(hs[0], on[0:4], S.hb1, T.bs[:, 384:512], T.bs[:, 384:512]),
+          (hs[1], on[4:8], S.hb1, T.bs[:, 384:512], T.bs[:, 384:512]),
+          (near[0], es, S.barr, T.bs[:, 0:128], T.bs[:, 384:512])])
     nb = 6 * len(es)
     g.wait_ge(S.aqd0, 1)
     g.wait_ge(S.aqd1, 1)
-    to_far(T.ps[:], T.as_[:], S.parr0)
-    to_far(codes(T.pq, 0, 256), codes(T.aq, 0, 256), S.parr0)
-    to_far(codes(T.pq, 256, 512), codes(T.aq, 256, 512), S.parr1)
-    nf = len(engines(far))
+    send([(hs[0], on[0:4], S.ha0, codes(T.aq, 0, 128), codes(T.aq, 0, 128)),
+          (hs[1], on[4:8], S.ha0, codes(T.aq, 128, 256), codes(T.aq, 128, 256)),
+          (far, es[0:4], S.parr0, codes(T.pq, 256, 384), codes(T.aq, 256, 384)),
+          (far, es[4:8], S.parr0, codes(T.pq, 384, 512), codes(T.aq, 384, 512))])
+    send([(hs[0], on[0:4], S.ha1, T.as_[:, 0:128], T.as_[:, 0:128]),
+          (hs[1], on[4:8], S.ha1, T.as_[:, 128:256], T.as_[:, 128:256]),
+          (far, es[0:4], S.parr0, T.ps[:, 256:384], T.as_[:, 256:384]),
+          (far, es[4:8], S.parr0, T.ps[:, 384:512], T.as_[:, 384:512])])
+    g.wait_ge(S.ones, 1)
+    g.affine_select(T.w[:], T.ones[:], [[-1, 516]], AluOpType.is_equal, 0.0, 3, 4).then_inc(S.wsel, 1)
 
     t = g.tensor
+
+    def product(own, i):
+        c = slice(128 * i, 128 * i + 128)
+        q, s, p, n = (T.aq, T.as_, T.pa, "p1_%d") if own else (T.pq, T.ps, T.pb, "p2_%d")
+        t.matmul_mx(p[:, 512 * i:512 * i + 512], q[:, c], s[:, c], T.bq[:], T.bs[:], True, True).then_inc(S[n % i], 1)
+
     t.wait_ge(S.bqd, 1)
     t.wait_ge(S.aqd0, 1)
     t.wait_ge(S.aqd1, 1)
     t.wait_ge(S.barr, nb)
-    for i in range(4):
-        c = slice(128 * i, 128 * i + 128)
-        t.matmul_mx(T.pa[:, 512 * i:512 * i + 512], T.aq[:, c], T.as_[:, c], T.bq[:], T.bs[:], True, True
-                    ).then_inc(S["p1_%d" % i], 1)
-    for i in range(4):
-        src, out = T.pa[:, 512 * i:512 * i + 512], T.h1[:, i:2048:4]
-        if i % 2 == 0:
-            g.scalar.wait_ge(S["p1_%d" % i], 1)
-            g.scalar.activation(out, src, ActivationFunctionType.Relu).then_inc(S["r1_%d" % i], 1)
-        else:
-            v.wait_ge(S["p1_%d" % i], 1)
-            v.tensor_scalar(out, src, 0.0, None, AluOpType.max).then_inc(S["r1_%d" % i], 1)
-    for i in range(4):
+    o = ORDER
+    product(True, o[0])
+    product(True, o[1])
+    t.wait_ge(S.parr0, 2 * len(es))
+    product(False, o[0])
+    product(True, o[2])
+    product(False, o[1])
+    product(True, o[3])
+    for i in o[2:]:
+        t.wait_ge(S["parr_%d" % i], 2 * len(es))
+        product(False, i)
+
+    sc = g.scalar
+
+    def clamp(own, i, lo, hi, sem):
+        src, out = (T.pa, T.r1) if own else (T.pb, T.r2)
+        sc.activation(out[:, 512 * i + lo:512 * i + hi], src[:, 512 * i + lo:512 * i + hi],
+                      ActivationFunctionType.Relu).then_inc(sem, 1)
+
+    v.wait_ge(S["p1_%d" % o[1]], 1)
+    v.tensor_scalar(T.r1[:, 512 * o[1]:512 * o[1] + 512], T.pa[:, 512 * o[1]:512 * o[1] + 512], 0.0, None, AluOpType.max
+                    ).then_inc(S["r1_%d" % o[1]], 1)
+    for own, i in ((True, o[0]), (False, o[0]), (True, o[2]), (False, o[1]), (True, o[3]), (False, o[2]), (False, o[3])):
+        sc.wait_ge(S[("p1_%d" if own else "p2_%d") % i], 1)
+        clamp(own, i, 0, 512 if own else 384, S[("r1_%d" if own else "r2_%d") % i])
+    for i in o:
+        clamp(False, i, 384, 512, S.ro)
+    for i in o:
         v.wait_ge(S["r1_%d" % i], 1)
-    v.quantize_mx(T.h1q[:], T.h1s[:], T.h1[:]).then_inc(S.h1d, 1)
-    t.wait_ge(S.sqd, 4)
-    t.wait_ge(S.h1d, 1)
-    for i in range(4):
-        c = slice(128 * i, 128 * i + 128)
-        t.matmul_mx(T.pb[:, 512 * i:512 * i + 512], T.sq[:, c], T.ss[:, c], T.h1q[:], T.h1s[:], True, False)
-    for i in range(4):
-        if i == 0:
-            t.wait_ge(S.parr0, 2 * nf)
-        if i == 2:
-            t.wait_ge(S.parr1, nf)
-        c = slice(128 * i, 128 * i + 128)
-        t.matmul_mx(T.pb[:, 512 * i:512 * i + 512], T.pq[:, c], T.ps[:, c], T.bq[:], T.bs[:], False, True
-                    ).then_inc(S["p2_%d" % i], 1)
-    for i in range(4):
-        v.wait_ge(S["p2_%d" % i], 1)
-        v.tensor_tensor(T.h2[:, i:1536:4], T.pb[:, 512 * i:512 * i + 384], T.h1[:, i:1536:4], AluOpType.max
+        v.wait_ge(S["r2_%d" % i], 1)
+        v.tensor_tensor(T.h2[:, i:1536:4], T.r1[:, 512 * i:512 * i + 384], T.r2[:, 512 * i:512 * i + 384], AluOpType.add
                         ).then_inc(S.h2m, 1)
     v.wait_ge(S.h2m, 4)
     v.quantize_mx(T.h2q[:], T.h2s[:], T.h2[:]).then_inc(S.h2d, 1)
+    v.wait_ge(S.wsel, 1)
     for i in range(4):
-        v.tensor_tensor(T.loc[:, i:512:4], T.pb[:, 512 * i + 384:512 * i + 512], T.h1[:, 1536 + i:2048:4], AluOpType.max
-                        ).then_inc(S.locd, 1)
+        v.quantize_mx(T.sq[:, 128 * i:128 * i + 128], T.ss[:, 128 * i:128 * i + 128],
+                      T.w[:, 3 - i:515 - i]).then_inc(S.sqd, 1)
+    v.wait_ge(S.ro, 4)
+    for i in range(4):
+        own = slice(512 * i + 384, 512 * i + 512)
+        v.tensor_tensor(T.loc[:, i:512:4], T.r1[:, own], T.r2[:, own], AluOpType.add).then_inc(S.locd, 1)
 
     mc = [es[0:4], es[4:6], es[6:8]]
     mp = [es[4:8], es[0:2], es[2:4]]
     g.wait_ge(S.h2d, 1)
-    for part, masks in ((0, mc), (1, mp)):
-        tr = []
-        for k in range(3):
-            lo, hi = 128 * k, 128 * k + 128
-            s, d = (codes(T.h2q, lo, hi), codes(T.uq, lo, hi)) if part == 0 else (T.h2s[:, lo:hi], T.us[:, lo:hi])
-            tr.append(RemoteDMATransfer(dst_ids=[ids[k]], dma_engine_mask=bits(masks[k]), remote_sem=S["t_%d" % k],
-                                        srcs=[s], dsts=[d]))
-            sent[0] += len(masks[k])
-        g.remote_dma_fused(tr, local_sem=S.sent)
+    send([(near[k], mc[k], S["t_%d" % k], codes(T.uq, 128 * k, 128 * k + 128), codes(T.h2q, 128 * k, 128 * k + 128))
+          for k in range(3)])
+    send([(near[k], mp[k], S["t_%d" % k], T.us[:, 128 * k:128 * k + 128], T.h2s[:, 128 * k:128 * k + 128])
+          for k in range(3)])
 
+    t.wait_ge(S.sqd, 4)
     for k in range(3):
         t.wait_ge(S["t_%d" % k], len(mc[k]) + len(mp[k]))
         u = slice(128 * k, 128 * k + 128)
         for i in range(4):
             c = slice(128 * i, 128 * i + 128)
+            if k == 0:
+                t.wait_ge(S["r1_%d" % i], 1)
             m = t.matmul_mx(T.pa[:, 512 * i:512 * i + 128], T.sq[:, c], T.ss[:, c], T.uq[:, u], T.us[:, u], k == 0, k == 2)
             if k == 2:
                 m.then_inc(S["u_%d" % i], 1)

@@ -4,36 +4,32 @@ from concourse.mybir import dt, AluOpType, ActivationFunctionType
 SCRATCH = {
     "a_in": ("sbuf", [128, 2048], "bfloat16"),
     "b_in": ("sbuf", [128, 512], "bfloat16"),
-    "aq": ("sbuf", [128, 512], "float8_e4m3fn_x4"),
-    "as_": ("sbuf", [128, 512], "uint8"),
-    "pq": ("sbuf", [128, 512], "float8_e4m3fn_x4"),
-    "ps": ("sbuf", [128, 512], "uint8"),
-    "bq": ("sbuf", [128, 512], "float8_e4m3fn_x4"),
-    "bs": ("sbuf", [128, 512], "uint8"),
+    "a_q": ("sbuf", [128, 512], "float8_e4m3fn_x4"),
+    "a_s": ("sbuf", [128, 512], "uint8"),
+    "p_q": ("sbuf", [128, 128], "float8_e4m3fn_x4"),
+    "p_s": ("sbuf", [128, 128], "uint8"),
+    "b_q": ("sbuf", [128, 512], "float8_e4m3fn_x4"),
+    "b_s": ("sbuf", [128, 512], "uint8"),
     "ones": ("sbuf", [128, 516], "bfloat16"),
     "w": ("sbuf", [128, 516], "bfloat16"),
-    "sq": ("sbuf", [128, 512], "float8_e4m3fn_x4"),
-    "ss": ("sbuf", [128, 512], "uint8"),
-    "r1": ("sbuf", [128, 2048], "float32"),
-    "r2": ("sbuf", [128, 2048], "float32"),
-    "h2": ("sbuf", [128, 1536], "bfloat16"),
-    "h2q": ("sbuf", [128, 384], "float8_e4m3fn_x4"),
-    "h2s": ("sbuf", [128, 384], "uint8"),
-    "uq": ("sbuf", [128, 384], "float8_e4m3fn_x4"),
-    "us": ("sbuf", [128, 384], "uint8"),
-    "loc": ("sbuf", [128, 512], "float32"),
+    "s_q": ("sbuf", [128, 256], "float8_e4m3fn_x4"),
+    "s_s": ("sbuf", [128, 256], "uint8"),
+    "h": ("sbuf", [128, 1024], "bfloat16"),
+    "u_q": ("sbuf", [128, 1216], "float8_e4m3fn_x4"),
+    "u_s": ("sbuf", [128, 1216], "uint8"),
     "yout": ("sbuf", [128, 512], "float32"),
-    "pa": ("psum", [128, 2048], "float32"),
-    "pb": ("psum", [128, 2048], "float32"),
+    "ps": ("psum", [128, 3072], "float32"),
 }
-SEMAPHORES = (["lb", "la0", "la1", "ones", "wsel", "bqd", "aqd0", "aqd1", "sqd", "barr", "parr0",
-               "h2m", "h2d", "locd", "yd", "st", "sent", "ro", "hb0", "hb1", "ha0", "ha1"]
-              + ["%s_%d" % (n, i) for n in ("p1", "r1", "p2", "r2", "u", "parr") for i in range(4)]
-              + ["t_%d" % k for k in range(3)])
-ORDER = (2, 3, 0, 1)
+SEMAPHORES = ["lb", "la0", "la1", "ones", "wsel", "bqd", "aqd", "sqd", "fb0", "fb1", "nb0", "nb1", "barr", "ta0", "ta1",
+              "to", "tp", "m0", "m1", "m2", "m3", "c0", "c1", "c2", "c3", "hd", "u0", "u1", "u2", "u3", "sa", "sb", "yd", "st",
+              "sent"]
 
 
-def around(r, T, topo):
+def bits(es):
+    return sum(1 << e for e in es)
+
+
+def cast(r, T, topo):
     near, far = [None, None, None], None
     for d in T.cores:
         if d == r:
@@ -42,52 +38,28 @@ def around(r, T, topo):
             near[0 if topo.mates(r, d) else 1 if topo.same_plane(r, d) else 2] = d
         elif topo.chip(d) == topo.chip(r) and topo.may_write(r, d):
             far = d
-    chip = [c for c in range(r - 128 if r > 128 else 0, r + 128)
+    chip = [c for c in range(max(0, r - 128), r + 128)
             if topo.host(c) == topo.host(r) and topo.chip(c) == topo.chip(r) and c != r]
-    ha = [c for c in chip if topo.die(c) == topo.die(r) and topo.may_write(c, near[1])][0]
-    hb = [c for c in chip if topo.die(c) != topo.die(r) and topo.may_write(c, near[2])][0]
-    return near, far, (ha, hb)
 
+    def part(same_die, port):
+        return [c for c in chip if (topo.die(c) == topo.die(r)) == same_die and topo.may_write(c, near[0]) == port]
 
-def bits(es):
-    return sum(1 << e for e in es)
-
-
-def codes(t, lo, hi):
-    return t[:, lo:hi].bitcast(dt.uint8)
-
-
-def helper(g, core, T, topo):
-    S = T.sem
-    for r in T.cores:
-        if topo.host(r) != topo.host(core) or topo.chip(r) != topo.chip(core):
-            continue
-        near, far, hs = around(r, T, topo)
-        if core not in hs:
-            continue
-        k = hs.index(core)
-        sent = 0
-        lo = 128 * k
-        n = 4
-        for sem, d, out, in_, rs in (
-                (S.hb0, near[1 + k], codes(T.bq, 128 + lo, 256 + lo), codes(T.bq, 384, 512), S.barr),
-                (S.hb1, near[1 + k], T.bs[:, 128 + lo:256 + lo], T.bs[:, 384:512], S.barr),
-                (S.ha0, far, codes(T.pq, lo, lo + 128), codes(T.aq, lo, lo + 128), S["parr_%d" % k]),
-                (S.ha1, far, T.ps[:, lo:lo + 128], T.as_[:, lo:lo + 128], S["parr_%d" % k])):
-            g.wait_ge(sem, n)
-            rid, pid = topo.addr(d, core)
-            m = topo.mask(core, d)
-            g.remote_dma(out, in_, rs, S.sent, pid, rid, m)
-            sent += sum(m >> e & 1 for e in range(16))
-        g.wait_ge(S.sent, sent)
+    comp = [r] + part(False, True) + part(True, True)
+    relay = {2: part(False, False)[0], 3: part(True, False)[0]}
+    return near, far, comp, relay, part(True, False)[1]
 
 
 def rank_program(g, core, T, topo):
-    if T.rank_of(core) is None:
-        helper(g, core, T, topo)
-        return
     S = T.sem
-    near, far, hs = around(core, T, topo)
+    r = [c for c in T.cores if topo.host(c) == topo.host(core) and topo.chip(c) == topo.chip(core)]
+    if not r:
+        return
+    r = r[0]
+    near, far, comp, relay, fwd = cast(r, T, topo)
+    ncast = [cast(d, T, topo) for d in near]
+    fcomp = cast(far, T, topo)[2]
+    if core not in comp and core not in relay.values() and core != fwd:
+        return
 
     def engines(d):
         m = topo.mask(core, d)
@@ -97,130 +69,150 @@ def rank_program(g, core, T, topo):
         rid, pid = topo.addr(d, core)
         return DstId(rid=rid, pnc=pid)
 
-    es = engines(near[0])
-    on = [e for e in engines(hs[0]) if e not in es]
+    es = engines(near[1])
+    on = [e for e in engines(comp[0] if core != comp[0] else fwd) if e not in es]
     sent = [0]
 
-    def send(transfers):
-        tr = []
-        for d, mask, sem, out, in_ in transfers:
-            tr.append(RemoteDMATransfer(dst_ids=[dst(d)], dma_engine_mask=bits(mask), remote_sem=sem, srcs=[in_], dsts=[out]))
-            sent[0] += len(mask)
-        g.remote_dma_fused(tr, local_sem=S.sent)
+    def move(items, waits=(None, None)):
+        for part in (0, 1):
+            tr = []
+            for ds, masks, sems, (ob, ol), (ib, il), n in items:
+                def view(b, lo):
+                    t = T[b + ("_q", "_s")[part]][:, lo:lo + n]
+                    return t.bitcast(dt.uint8) if part == 0 else t
+                tr.append(RemoteDMATransfer(dst_ids=[dst(d) for d in ds], dma_engine_mask=bits(masks[part]),
+                                            remote_sem=S[sems[part]], srcs=[view(ib, il)], dsts=[view(ob, ol) for d in ds]))
+                sent[0] += len(masks[part])
+            if waits[part]:
+                g.wait_ge(S[waits[part][0]], waits[part][1])
+            g.remote_dma_fused(tr, local_sem=S.sent)
 
-    g.sync.dma_start(T.b_in[:], T.b[:]).then_inc(S.lb, 16)
-    g.scalar.dma_start(T.a_in[:, 0:1024], T.a[:, 0:1024]).then_inc(S.la0, 16)
-    g.sync.dma_start(T.a_in[:, 1024:2048], T.a[:, 1024:2048]).then_inc(S.la1, 16)
+    def both(x):
+        return (x, x)
 
-    v = g.vector
-    v.memset(T.ones[:], 1.0).then_inc(S.ones, 1)
-    v.wait_ge(S.lb, 16)
-    v.quantize_mx(T.bq[:, 384:512], T.bs[:, 384:512], T.b_in[:]).then_inc(S.bqd, 1)
-    v.wait_ge(S.la0, 16)
-    v.quantize_mx(T.aq[:, 0:256], T.as_[:, 0:256], T.a_in[:, 0:1024]).then_inc(S.aqd0, 1)
-    v.wait_ge(S.la1, 16)
-    v.quantize_mx(T.aq[:, 256:512], T.as_[:, 256:512], T.a_in[:, 1024:2048]).then_inc(S.aqd1, 1)
+    def b_on(slot, ds, masks, sems, here=None):
+        return (ds, both(masks), sems, ("b", 128 * slot), ("b", 128 * (slot if here is None else here)), 128)
 
-    g.wait_ge(S.bqd, 1)
-    send([(hs[0], on[0:4], S.hb0, codes(T.bq, 384, 512), codes(T.bq, 384, 512)),
-          (hs[1], on[4:8], S.hb0, codes(T.bq, 384, 512), codes(T.bq, 384, 512)),
-          (near[0], es, S.barr, codes(T.bq, 0, 128), codes(T.bq, 384, 512))])
-    send([(hs[0], on[0:4], S.hb1, T.bs[:, 384:512], T.bs[:, 384:512]),
-          (hs[1], on[4:8], S.hb1, T.bs[:, 384:512], T.bs[:, 384:512]),
-          (near[0], es, S.barr, T.bs[:, 0:128], T.bs[:, 384:512])])
-    nb = 6 * len(es)
-    g.wait_ge(S.aqd0, 1)
-    g.wait_ge(S.aqd1, 1)
-    send([(hs[0], on[0:4], S.ha0, codes(T.aq, 0, 128), codes(T.aq, 0, 128)),
-          (hs[1], on[4:8], S.ha0, codes(T.aq, 128, 256), codes(T.aq, 128, 256)),
-          (far, es[0:4], S.parr0, codes(T.pq, 256, 384), codes(T.aq, 256, 384)),
-          (far, es[4:8], S.parr0, codes(T.pq, 384, 512), codes(T.aq, 384, 512))])
-    send([(hs[0], on[0:4], S.ha1, T.as_[:, 0:128], T.as_[:, 0:128]),
-          (hs[1], on[4:8], S.ha1, T.as_[:, 128:256], T.as_[:, 128:256]),
-          (far, es[0:4], S.parr0, T.ps[:, 256:384], T.as_[:, 256:384]),
-          (far, es[4:8], S.parr0, T.ps[:, 384:512], T.as_[:, 384:512])])
-    g.wait_ge(S.ones, 1)
-    g.affine_select(T.w[:], T.ones[:], [[-1, 516]], AluOpType.is_equal, 0.0, 3, 4).then_inc(S.wsel, 1)
+    half = len(es) // 2
+    FB, NB, TA, BA = ("fb0", "fb1"), ("nb0", "nb1"), ("ta0", "ta1"), both("barr")
+    q = comp.index(core) if core in comp else None
+    wait_b, wait_own, n_tp = [], [], 2 * len(es)
+    fan = 2 * (len(es) + len(on))
+    v, t, sc = g.vector, g.tensor, g.scalar
 
-    t = g.tensor
+    if q == 0:
+        g.sync.dma_start(T.b_in[:], T.b[:]).then_inc(S.lb, 16)
+        sc.dma_start(T.a_in[:, 0:1024], T.a[:, 0:1024]).then_inc(S.la0, 16)
+        g.sync.dma_start(T.a_in[:, 1024:2048], T.a[:, 1024:2048]).then_inc(S.la1, 16)
+        v.memset(T.ones[:], 1.0).then_inc(S.ones, 1)
+        v.wait_ge(S.lb, 16)
+        v.quantize_mx(T.b_q[:, 384:512], T.b_s[:, 384:512], T.b_in[:]).then_inc(S.bqd, 1)
+        for i, s in ((0, S.la0), (1, S.la1)):
+            v.wait_ge(s, 16)
+            v.quantize_mx(T.a_q[:, 256 * i:256 * i + 256], T.a_s[:, 256 * i:256 * i + 256],
+                          T.a_in[:, 1024 * i:1024 * i + 1024]).then_inc(S.aqd, 1)
+        g.wait_ge(S.bqd, 1)
+        move([b_on(3, [comp[2]], on[:half], FB), b_on(3, [fwd], on[half:], FB),
+              b_on(0, [ncast[0][2][3]], es, NB, 3)])
+        g.wait_ge(S.aqd, 2)
+        move([([fcomp[0]], both(es[:half]), both("tp"), ("p", 0), ("a", 0), 128),
+              ([comp[1]], both(es[half:]), TA, ("a", 0), ("a", 128), 128),
+              ([relay[2]], both(on[:half]), TA, ("a", 0), ("a", 256), 128),
+              ([relay[3]], both(on[half:]), TA, ("a", 0), ("a", 384), 128)])
+        g.wait_ge(S.ones, 1)
+        g.affine_select(T.w[:], T.ones[:], [[-1, 258], [0, 2]], AluOpType.is_equal, 0.0, 1, 2).then_inc(S.wsel, 1)
+        v.wait_ge(S.wsel, 1)
+        for i in range(2):
+            v.quantize_mx(T.s_q[:, 128 * i:128 * i + 128], T.s_s[:, 128 * i:128 * i + 128],
+                          T.w[:, 2 - 2 * i:514 - 2 * i]).then_inc(S.sqd, 1)
+        wait_b = [(S.bqd, 1), (S.barr, 3 * fan)]
+        wait_own = [(S.aqd, 2)]
+        n_tp = 2 * half
+    elif q == 1:
+        move([([fcomp[1]], both(es), both("tp"), ("p", 0), ("a", 0), 128)], (("ta0", half), ("ta1", half)))
+        wait_b = [(S.barr, 3 * fan + 2 * len(on))]
+        wait_own = [(S.ta0, half), (S.ta1, half)]
+    elif q == 2:
+        move([b_on(2, [ncast[2][2][2]], es, NB, 3)], (("fb0", half), ("fb1", half)))
+        move([b_on(3, [comp[3]], on, BA)])
+        move([b_on(2, [comp[0], comp[1], comp[3]], es + on, BA)], (("nb0", len(es)), ("nb1", len(es))))
+        wait_b = [(S.fb0, half), (S.fb1, half), (S.nb0, len(es)), (S.nb1, len(es)), (S.barr, 2 * fan)]
+    elif q == 3:
+        move([b_on(0, [comp[0], comp[1], comp[2]], es + on, BA)], (("nb0", len(es)), ("nb1", len(es))))
+        wait_b = [(S.nb0, len(es)), (S.nb1, len(es)), (S.barr, 2 * fan + 2 * len(on))]
+    elif core == fwd:
+        move([b_on(1, [ncast[1][4]], es, NB, 3)], (("fb0", half), ("fb1", half)))
+        move([b_on(3, [comp[1]], on, BA)])
+        move([b_on(1, comp, es + on, BA)], (("nb0", len(es)), ("nb1", len(es))))
+    else:
+        k = [i for i in relay if relay[i] == core][0]
+        move([([fcomp[k]], both(es), both("tp"), ("p", 0), ("a", 0), 128)], (("ta0", half), ("ta1", half)))
+        move([([comp[k]], both(on), both("to"), ("a", 0), ("a", 0), 128)])
+    if q is None:
+        g.wait_ge(S.sent, sent[0])
+        return
+    if q >= 2:
+        wait_own = [(S.to, 2 * len(on))]
 
-    def product(own, i):
-        c = slice(128 * i, 128 * i + 128)
-        q, s, p, n = (T.aq, T.as_, T.pa, "p1_%d") if own else (T.pq, T.ps, T.pb, "p2_%d")
-        t.matmul_mx(p[:, 512 * i:512 * i + 512], q[:, c], s[:, c], T.bq[:], T.bs[:], True, True).then_inc(S[n % i], 1)
+    for s, n in wait_b + wait_own:
+        t.wait_ge(s, n)
+    for src in (0, 1):
+        if src == 1:
+            t.wait_ge(S.tp, n_tp)
+        for hf in (0, 1):
+            j = 2 * src + hf
+            w = "ap"[src]
+            t.matmul_mx(T.ps[:, 512 * j:512 * j + 256], T[w + "_q"][:, 0:128], T[w + "_s"][:, 0:128],
+                        T.b_q[:, 256 * hf:256 * hf + 256], T.b_s[:, 256 * hf:256 * hf + 256], True, True
+                        ).then_inc(S["m%d" % j], 1)
+    for src in (0, 1):
+        for hf in (0, 1):
+            j = 2 * src + hf
+            out = T.h[:, 512 * hf + src:512 * hf + 512:2]
+            in_ = T.ps[:, 512 * j:512 * j + 256]
+            if hf == 0:
+                v.wait_ge(S["m%d" % j], 1)
+                v.tensor_scalar(out, in_, 0.0, None, AluOpType.max).then_inc(S["c%d" % j], 1)
+            else:
+                sc.wait_ge(S["m%d" % j], 1)
+                sc.activation(out, in_, ActivationFunctionType.Relu).then_inc(S["c%d" % j], 1)
+    for hf in (0, 1):
+        v.wait_ge(S["c%d" % hf], 1)
+        v.wait_ge(S["c%d" % (2 + hf)], 1)
+        v.quantize_mx(T.u_q[:, 128 * hf:128 * hf + 128], T.u_s[:, 128 * hf:128 * hf + 128],
+                      T.h[:, 512 * hf:512 * hf + 512]).then_inc(S.hd, 1)
 
-    t.wait_ge(S.bqd, 1)
-    t.wait_ge(S.aqd0, 1)
-    t.wait_ge(S.aqd1, 1)
-    t.wait_ge(S.barr, nb)
-    o = ORDER
-    product(True, o[0])
-    product(True, o[1])
-    t.wait_ge(S.parr0, 2 * len(es))
-    product(False, o[0])
-    product(True, o[2])
-    product(False, o[1])
-    product(True, o[3])
-    for i in o[2:]:
-        t.wait_ge(S["parr_%d" % i], 2 * len(es))
-        product(False, i)
+    quarter = len(es) // 4
+    mc = [es[:half], es[half:half + quarter], es[half + quarter:]]
+    mp = [es[half:], es[:quarter], es[quarter:half]]
+    items = [([near[k]], (mc[k], mp[k]), both("u%d" % k), ("u", 448 + 256 * k + 64 * q), ("u", 64 * k), 64) for k in range(3)]
+    own = {1: on[:half], 2: on, 3: on}
+    if q:
+        items.append(([comp[0]], both(own[q]), both("u3"), ("u", 192 + 64 * q), ("u", 192), 64))
+    g.wait_ge(S.hd, 2)
+    move(items)
 
-    sc = g.scalar
-
-    def clamp(own, i, lo, hi, sem):
-        src, out = (T.pa, T.r1) if own else (T.pb, T.r2)
-        sc.activation(out[:, 512 * i + lo:512 * i + hi], src[:, 512 * i + lo:512 * i + hi],
-                      ActivationFunctionType.Relu).then_inc(sem, 1)
-
-    v.wait_ge(S["p1_%d" % o[1]], 1)
-    v.tensor_scalar(T.r1[:, 512 * o[1]:512 * o[1] + 512], T.pa[:, 512 * o[1]:512 * o[1] + 512], 0.0, None, AluOpType.max
-                    ).then_inc(S["r1_%d" % o[1]], 1)
-    for own, i in ((True, o[0]), (False, o[0]), (True, o[2]), (False, o[1]), (True, o[3]), (False, o[2]), (False, o[3])):
-        sc.wait_ge(S[("p1_%d" if own else "p2_%d") % i], 1)
-        clamp(own, i, 0, 512 if own else 384, S[("r1_%d" if own else "r2_%d") % i])
-    for i in o:
-        clamp(False, i, 384, 512, S.ro)
-    for i in o:
-        v.wait_ge(S["r1_%d" % i], 1)
-        v.wait_ge(S["r2_%d" % i], 1)
-        v.tensor_tensor(T.h2[:, i:1536:4], T.r1[:, 512 * i:512 * i + 384], T.r2[:, 512 * i:512 * i + 384], AluOpType.add
-                        ).then_inc(S.h2m, 1)
-    v.wait_ge(S.h2m, 4)
-    v.quantize_mx(T.h2q[:], T.h2s[:], T.h2[:]).then_inc(S.h2d, 1)
-    v.wait_ge(S.wsel, 1)
-    for i in range(4):
-        v.quantize_mx(T.sq[:, 128 * i:128 * i + 128], T.ss[:, 128 * i:128 * i + 128],
-                      T.w[:, 3 - i:515 - i]).then_inc(S.sqd, 1)
-    v.wait_ge(S.ro, 4)
-    for i in range(4):
-        own = slice(512 * i + 384, 512 * i + 512)
-        v.tensor_tensor(T.loc[:, i:512:4], T.r1[:, own], T.r2[:, own], AluOpType.add).then_inc(S.locd, 1)
-
-    mc = [es[0:4], es[4:6], es[6:8]]
-    mp = [es[4:8], es[0:2], es[2:4]]
-    g.wait_ge(S.h2d, 1)
-    send([(near[k], mc[k], S["t_%d" % k], codes(T.uq, 128 * k, 128 * k + 128), codes(T.h2q, 128 * k, 128 * k + 128))
-          for k in range(3)])
-    send([(near[k], mp[k], S["t_%d" % k], T.us[:, 128 * k:128 * k + 128], T.h2s[:, 128 * k:128 * k + 128])
-          for k in range(3)])
-
-    t.wait_ge(S.sqd, 4)
-    for k in range(3):
-        t.wait_ge(S["t_%d" % k], len(mc[k]) + len(mp[k]))
-        u = slice(128 * k, 128 * k + 128)
+    if q == 0:
+        t.wait_ge(S.sqd, 2)
+        t.wait_ge(S.hd, 2)
+        order = (3, 0, 1, 2)
+        for k in order:
+            n = 2 * sum(len(own[i]) for i in own) if k == 3 else len(comp) * (len(mc[k]) + len(mp[k]))
+            t.wait_ge(S["u%d" % k], n)
+            lo = 192 if k == 3 else 448 + 256 * k
+            for i in (0, 1):
+                c = slice(128 * i, 128 * i + 128)
+                m = t.matmul_mx(T.ps[:, 2048 + 512 * i:2304 + 512 * i], T.s_q[:, c], T.s_s[:, c],
+                                T.u_q[:, lo:lo + 256], T.u_s[:, lo:lo + 256], k == order[0], k == order[-1])
+                if k == order[-1]:
+                    m.then_inc(S["s" + "ab"[i]], 1)
+        v.wait_ge(S.sa, 1)
+        sc.wait_ge(S.sb, 1)
         for i in range(4):
-            c = slice(128 * i, 128 * i + 128)
-            if k == 0:
-                t.wait_ge(S["r1_%d" % i], 1)
-            m = t.matmul_mx(T.pa[:, 512 * i:512 * i + 128], T.sq[:, c], T.ss[:, c], T.uq[:, u], T.us[:, u], k == 0, k == 2)
-            if k == 2:
-                m.then_inc(S["u_%d" % i], 1)
-    v.wait_ge(S.locd, 4)
-    for i in range(4):
-        v.wait_ge(S["u_%d" % i], 1)
-        v.tensor_tensor(T.yout[:, i:512:4], T.pa[:, 512 * i:512 * i + 128], T.loc[:, i:512:4], AluOpType.add
-                        ).then_inc(S.yd, 1)
-    g.sync.wait_ge(S.yd, 4)
-    g.sync.dma_start(T.y[:], T.yout[:]).then_inc(S.st, 16)
-    g.sync.wait_ge(S.st, 16)
+            v.tensor_copy(T.yout[:, i:512:8], T.ps[:, 2048 + 64 * i:2112 + 64 * i]).then_inc(S.yd, 1)
+            sc.activation(T.yout[:, 4 + i:512:8], T.ps[:, 2560 + 64 * i:2624 + 64 * i], ActivationFunctionType.Copy
+                          ).then_inc(S.yd, 1)
+        g.sync.wait_ge(S.yd, 8)
+        g.sync.dma_start(T.y[:], T.yout[:]).then_inc(S.st, 16)
+        g.sync.wait_ge(S.st, 16)
     g.wait_ge(S.sent, sent[0])

from concourse.bass import DstId, RemoteDMATransfer
from concourse.mybir import dt, AluOpType, ActivationFunctionType

SCRATCH = {
    "a_in": ("sbuf", [128, 2048], "bfloat16"),
    "b_in": ("sbuf", [128, 512], "bfloat16"),
    "a_q": ("sbuf", [128, 512], "float8_e4m3fn_x4"),
    "a_s": ("sbuf", [128, 512], "uint8"),
    "p_q": ("sbuf", [128, 128], "float8_e4m3fn_x4"),
    "p_s": ("sbuf", [128, 128], "uint8"),
    "b_q": ("sbuf", [128, 512], "float8_e4m3fn_x4"),
    "b_s": ("sbuf", [128, 512], "uint8"),
    "ones": ("sbuf", [128, 516], "bfloat16"),
    "w": ("sbuf", [128, 516], "bfloat16"),
    "s_q": ("sbuf", [128, 256], "float8_e4m3fn_x4"),
    "s_s": ("sbuf", [128, 256], "uint8"),
    "h": ("sbuf", [128, 1024], "bfloat16"),
    "u_q": ("sbuf", [128, 1216], "float8_e4m3fn_x4"),
    "u_s": ("sbuf", [128, 1216], "uint8"),
    "yout": ("sbuf", [128, 512], "float32"),
    "ps": ("psum", [128, 3072], "float32"),
}
SEMAPHORES = ["lb", "la0", "la1", "ones", "wsel", "bqd", "aqd", "sqd", "fb0", "fb1", "nb0", "nb1", "barr", "ta0", "ta1",
              "to", "tp", "m0", "m1", "m2", "m3", "c0", "c1", "c2", "c3", "hd", "u0", "u1", "u2", "u3", "sa", "sb", "yd", "st",
              "sent"]


def bits(es):
    return sum(1 << e for e in es)


def cast(r, T, topo):
    near, far = [None, None, None], None
    for d in T.cores:
        if d == r:
            continue
        if topo.rack(topo.host(d)) == topo.rack(topo.host(r)):
            near[0 if topo.mates(r, d) else 1 if topo.same_plane(r, d) else 2] = d
        elif topo.chip(d) == topo.chip(r) and topo.may_write(r, d):
            far = d
    chip = [c for c in range(max(0, r - 128), r + 128)
            if topo.host(c) == topo.host(r) and topo.chip(c) == topo.chip(r) and c != r]

    def part(same_die, port):
        return [c for c in chip if (topo.die(c) == topo.die(r)) == same_die and topo.may_write(c, near[0]) == port]

    comp = [r] + part(False, True) + part(True, True)
    relay = {2: part(False, False)[0], 3: part(True, False)[0]}
    return near, far, comp, relay, part(True, False)[1]


def rank_program(g, core, T, topo):
    S = T.sem
    r = [c for c in T.cores if topo.host(c) == topo.host(core) and topo.chip(c) == topo.chip(core)]
    if not r:
        return
    r = r[0]
    near, far, comp, relay, fwd = cast(r, T, topo)
    ncast = [cast(d, T, topo) for d in near]
    fcomp = cast(far, T, topo)[2]
    if core not in comp and core not in relay.values() and core != fwd:
        return

    def engines(d):
        m = topo.mask(core, d)
        return [e for e in range(16) if m >> e & 1]

    def dst(d):
        rid, pid = topo.addr(d, core)
        return DstId(rid=rid, pnc=pid)

    es = engines(near[1])
    on = [e for e in engines(comp[0] if core != comp[0] else fwd) if e not in es]
    sent = [0]

    def move(items, waits=(None, None)):
        for part in (0, 1):
            tr = []
            for ds, masks, sems, (ob, ol), (ib, il), n in items:
                def view(b, lo):
                    t = T[b + ("_q", "_s")[part]][:, lo:lo + n]
                    return t.bitcast(dt.uint8) if part == 0 else t
                tr.append(RemoteDMATransfer(dst_ids=[dst(d) for d in ds], dma_engine_mask=bits(masks[part]),
                                            remote_sem=S[sems[part]], srcs=[view(ib, il)], dsts=[view(ob, ol) for d in ds]))
                sent[0] += len(masks[part])
            if waits[part]:
                g.wait_ge(S[waits[part][0]], waits[part][1])
            g.remote_dma_fused(tr, local_sem=S.sent)

    def both(x):
        return (x, x)

    def b_on(slot, ds, masks, sems, here=None):
        return (ds, both(masks), sems, ("b", 128 * slot), ("b", 128 * (slot if here is None else here)), 128)

    half = len(es) // 2
    FB, NB, TA, BA = ("fb0", "fb1"), ("nb0", "nb1"), ("ta0", "ta1"), both("barr")
    q = comp.index(core) if core in comp else None
    wait_b, wait_own, n_tp = [], [], 2 * len(es)
    fan = 2 * (len(es) + len(on))
    v, t, sc = g.vector, g.tensor, g.scalar

    if q == 0:
        g.sync.dma_start(T.b_in[:], T.b[:]).then_inc(S.lb, 16)
        sc.dma_start(T.a_in[:, 0:1024], T.a[:, 0:1024]).then_inc(S.la0, 16)
        g.sync.dma_start(T.a_in[:, 1024:2048], T.a[:, 1024:2048]).then_inc(S.la1, 16)
        v.memset(T.ones[:], 1.0).then_inc(S.ones, 1)
        v.wait_ge(S.lb, 16)
        v.quantize_mx(T.b_q[:, 384:512], T.b_s[:, 384:512], T.b_in[:]).then_inc(S.bqd, 1)
        for i, s in ((0, S.la0), (1, S.la1)):
            v.wait_ge(s, 16)
            v.quantize_mx(T.a_q[:, 256 * i:256 * i + 256], T.a_s[:, 256 * i:256 * i + 256],
                          T.a_in[:, 1024 * i:1024 * i + 1024]).then_inc(S.aqd, 1)
        g.wait_ge(S.bqd, 1)
        move([b_on(3, [comp[2]], on[:half], FB), b_on(3, [fwd], on[half:], FB),
              b_on(0, [ncast[0][2][3]], es, NB, 3)])
        g.wait_ge(S.aqd, 2)
        move([([fcomp[0]], both(es[:half]), both("tp"), ("p", 0), ("a", 0), 128),
              ([comp[1]], both(es[half:]), TA, ("a", 0), ("a", 128), 128),
              ([relay[2]], both(on[:half]), TA, ("a", 0), ("a", 256), 128),
              ([relay[3]], both(on[half:]), TA, ("a", 0), ("a", 384), 128)])
        g.wait_ge(S.ones, 1)
        g.affine_select(T.w[:], T.ones[:], [[-1, 258], [0, 2]], AluOpType.is_equal, 0.0, 1, 2).then_inc(S.wsel, 1)
        v.wait_ge(S.wsel, 1)
        for i in range(2):
            v.quantize_mx(T.s_q[:, 128 * i:128 * i + 128], T.s_s[:, 128 * i:128 * i + 128],
                          T.w[:, 2 - 2 * i:514 - 2 * i]).then_inc(S.sqd, 1)
        wait_b = [(S.bqd, 1), (S.barr, 3 * fan)]
        wait_own = [(S.aqd, 2)]
        n_tp = 2 * half
    elif q == 1:
        move([([fcomp[1]], both(es), both("tp"), ("p", 0), ("a", 0), 128)], (("ta0", half), ("ta1", half)))
        wait_b = [(S.barr, 3 * fan + 2 * len(on))]
        wait_own = [(S.ta0, half), (S.ta1, half)]
    elif q == 2:
        move([b_on(2, [ncast[2][2][2]], es, NB, 3)], (("fb0", half), ("fb1", half)))
        move([b_on(3, [comp[3]], on, BA)])
        move([b_on(2, [comp[0], comp[1], comp[3]], es + on, BA)], (("nb0", len(es)), ("nb1", len(es))))
        wait_b = [(S.fb0, half), (S.fb1, half), (S.nb0, len(es)), (S.nb1, len(es)), (S.barr, 2 * fan)]
    elif q == 3:
        move([b_on(0, [comp[0], comp[1], comp[2]], es + on, BA)], (("nb0", len(es)), ("nb1", len(es))))
        wait_b = [(S.nb0, len(es)), (S.nb1, len(es)), (S.barr, 2 * fan + 2 * len(on))]
    elif core == fwd:
        move([b_on(1, [ncast[1][4]], es, NB, 3)], (("fb0", half), ("fb1", half)))
        move([b_on(3, [comp[1]], on, BA)])
        move([b_on(1, comp, es + on, BA)], (("nb0", len(es)), ("nb1", len(es))))
    else:
        k = [i for i in relay if relay[i] == core][0]
        move([([fcomp[k]], both(es), both("tp"), ("p", 0), ("a", 0), 128)], (("ta0", half), ("ta1", half)))
        move([([comp[k]], both(on), both("to"), ("a", 0), ("a", 0), 128)])
    if q is None:
        g.wait_ge(S.sent, sent[0])
        return
    if q >= 2:
        wait_own = [(S.to, 2 * len(on))]

    for s, n in wait_b + wait_own:
        t.wait_ge(s, n)
    for src in (0, 1):
        if src == 1:
            t.wait_ge(S.tp, n_tp)
        for hf in (0, 1):
            j = 2 * src + hf
            w = "ap"[src]
            t.matmul_mx(T.ps[:, 512 * j:512 * j + 256], T[w + "_q"][:, 0:128], T[w + "_s"][:, 0:128],
                        T.b_q[:, 256 * hf:256 * hf + 256], T.b_s[:, 256 * hf:256 * hf + 256], True, True
                        ).then_inc(S["m%d" % j], 1)
    for src in (0, 1):
        for hf in (0, 1):
            j = 2 * src + hf
            out = T.h[:, 512 * hf + src:512 * hf + 512:2]
            in_ = T.ps[:, 512 * j:512 * j + 256]
            if hf == 0:
                v.wait_ge(S["m%d" % j], 1)
                v.tensor_scalar(out, in_, 0.0, None, AluOpType.max).then_inc(S["c%d" % j], 1)
            else:
                sc.wait_ge(S["m%d" % j], 1)
                sc.activation(out, in_, ActivationFunctionType.Relu).then_inc(S["c%d" % j], 1)
    for hf in (0, 1):
        v.wait_ge(S["c%d" % hf], 1)
        v.wait_ge(S["c%d" % (2 + hf)], 1)
        v.quantize_mx(T.u_q[:, 128 * hf:128 * hf + 128], T.u_s[:, 128 * hf:128 * hf + 128],
                      T.h[:, 512 * hf:512 * hf + 512]).then_inc(S.hd, 1)

    quarter = len(es) // 4
    mc = [es[:half], es[half:half + quarter], es[half + quarter:]]
    mp = [es[half:], es[:quarter], es[quarter:half]]
    items = [([near[k]], (mc[k], mp[k]), both("u%d" % k), ("u", 448 + 256 * k + 64 * q), ("u", 64 * k), 64) for k in range(3)]
    own = {1: on[:half], 2: on, 3: on}
    if q:
        items.append(([comp[0]], both(own[q]), both("u3"), ("u", 192 + 64 * q), ("u", 192), 64))
    g.wait_ge(S.hd, 2)
    move(items)

    if q == 0:
        t.wait_ge(S.sqd, 2)
        t.wait_ge(S.hd, 2)
        order = (3, 0, 1, 2)
        for k in order:
            n = 2 * sum(len(own[i]) for i in own) if k == 3 else len(comp) * (len(mc[k]) + len(mp[k]))
            t.wait_ge(S["u%d" % k], n)
            lo = 192 if k == 3 else 448 + 256 * k
            for i in (0, 1):
                c = slice(128 * i, 128 * i + 128)
                m = t.matmul_mx(T.ps[:, 2048 + 512 * i:2304 + 512 * i], T.s_q[:, c], T.s_s[:, c],
                                T.u_q[:, lo:lo + 256], T.u_s[:, lo:lo + 256], k == order[0], k == order[-1])
                if k == order[-1]:
                    m.then_inc(S["s" + "ab"[i]], 1)
        v.wait_ge(S.sa, 1)
        sc.wait_ge(S.sb, 1)
        for i in range(4):
            v.tensor_copy(T.yout[:, i:512:8], T.ps[:, 2048 + 64 * i:2112 + 64 * i]).then_inc(S.yd, 1)
            sc.activation(T.yout[:, 4 + i:512:8], T.ps[:, 2560 + 64 * i:2624 + 64 * i], ActivationFunctionType.Copy
                          ).then_inc(S.yd, 1)
        g.sync.wait_ge(S.yd, 8)
        g.sync.dma_start(T.y[:], T.yout[:]).then_inc(S.st, 16)
        g.sync.wait_ge(S.st, 16)
    g.wait_ge(S.sent, sent[0])
